import numpy as np
import ml_dtypes


def mxq(x, axis, fmt="e4m3"):
    dtype, down = {"e4m3": (ml_dtypes.float8_e4m3fn, 7), "e5m2": (ml_dtypes.float8_e5m2, 14)}[fmt]
    v = np.moveaxis(np.asarray(x, np.float32).astype(ml_dtypes.bfloat16).astype(np.float64), axis, -1)
    blocks = v.reshape(v.shape[:-1] + (-1, 32))
    amax = np.abs(blocks).max(-1, keepdims=True)
    byte = np.maximum(np.where(amax > 0, np.frexp(amax)[1] - 1 + 127, 0) - down, 1)
    scale = np.exp2(byte - 127.0)
    codes = (blocks / scale).astype(np.float32).astype(dtype).astype(np.float64)
    return np.moveaxis((codes * scale).reshape(v.shape), -1, axis)


WIDE = False


def mx_kscale(k):
    if not WIDE:
        return np.ones(k)
    levels = np.array([10, -10, 5, -5, 0])
    if k % 512:
        return np.exp2(np.random.permutation(np.resize(levels, k // 32))).repeat(32)
    a = np.empty((k // 512, 16))
    for p in range(k // 512):
        a[p, :8] = np.random.permutation(np.resize(levels, 8))
        for g in range(8):
            far = levels[np.abs(levels - a[p, g]) >= 10]
            a[p, g + 8] = far[np.random.randint(len(far))]
    return np.exp2(a.ravel()).repeat(32)


def f64(x):
    return np.asarray(x).astype(np.float64)


def striped8(idx):
    return np.concatenate([v.reshape(-1, 16).T for v in idx]).astype(np.uint16)


def unstriped8(offs):
    return np.stack([offs[16 * g:16 * g + 16].T.reshape(-1) for g in range(8)]).astype(np.int64)


E2M1 = np.array([0.0, 0.5, 1.0, 1.5, 2.0, 3.0, 4.0, 6.0, -0.0, -0.5, -1.0, -1.5, -2.0, -3.0, -4.0, -6.0])


def pack_weight(w, fmt):
    k, n = w.shape
    w = f64(np.asarray(w, np.float32).astype(ml_dtypes.bfloat16)).reshape(k // 32, 32, n)
    amax = np.abs(w).max(1)
    if fmt == "e4m3":
        byte = np.frexp(amax)[1] - 1 + 127 - 7
    else:
        mant, ex = np.frexp(amax / 6.0)
        byte = np.where(mant > 0.5, ex, ex - 1) + 127
    byte = np.clip(np.where(amax > 0, byte, 1), 1, 254)
    scaled = (w * np.exp2(127.0 - byte)[:, None, :]).reshape(k, n).astype(np.float32)
    by_word = np.ascontiguousarray(scaled.reshape(k // 512, 128, 4, n).transpose(0, 1, 3, 2))
    if fmt == "e4m3":
        words = by_word.astype(ml_dtypes.float8_e4m3fn).view(np.uint8)
    else:
        c = by_word.astype(ml_dtypes.float4_e2m1fn).view(np.uint8) & 0xF
        words = (c[..., 0::2] | (c[..., 1::2] << 4)).reshape(k // 512, 128, 2 * n)
    return np.ascontiguousarray(words), np.ascontiguousarray(byte.astype(np.uint8).reshape(k // 512, 16, n))


def unpack_weight(words, scales, fmt):
    g, _, n = scales.shape
    words = np.ascontiguousarray(words).reshape(g, 128, n, -1)
    if fmt == "e4m3":
        vals = words.view(ml_dtypes.float8_e4m3fn).astype(np.float64)
    else:
        nib = np.empty((g, 128, n, 4), np.uint8)
        nib[..., 0::2] = words & 0xF
        nib[..., 1::2] = words >> 4
        vals = E2M1[nib]
    vals = vals * np.repeat(np.exp2(scales.astype(np.float64) - 127.0), 8, axis=1)[..., None]
    return vals.transpose(0, 1, 3, 2).reshape(g * 512, n)


K, M, T, S = 512, 256, 2048, 512


def setup_inputs():
    n = np.random.standard_normal
    s = mx_kscale(K)[:, None]
    w = n((K, M)) / np.sqrt(K) / s
    w4 = pack_weight(w, "e2m1")
    rest = w - unpack_weight(*w4, "e2m1")
    p_r8 = pack_weight(rest, "e4m3")
    return {
        "xT": (n((K, T)) * s).astype(np.float32),
        "w4_words": w4[0],
        "w4_scales": w4[1],
        "r8_words": p_r8[0],
        "r8_scales": p_r8[1],
        "wgt": np.repeat(np.random.uniform(0.5, 2.0, (8, S)), 16, axis=0).astype(np.float32),
        "b": (0.3 * n(256)).astype(np.float32),
        "offs": striped8(np.stack([np.random.permutation(T)[:S] for _ in range(8)])),
    }


def reference(xT, w4_words, w4_scales, r8_words, r8_scales, wgt, b, offs):
    idx = unstriped8(offs)
    group = np.arange(K) % 512 // 64
    xg = f64(wgt)[np.arange(K) // 4 % 128] * f64(xT)[np.arange(K)[:, None], idx[group]]
    xT_ = mxq(xg, 0, "e4m3")
    w4_ = unpack_weight(w4_words, w4_scales, "e2m1")
    r8_ = unpack_weight(r8_words, r8_scales, "e4m3")
    y = xT_.T @ w4_ + xT_.T @ r8_
    return y + f64(b)[None, :]

@@ -1,0 +1,132 @@
+from contextlib import ExitStack
+
+import concourse.mybir as mybir
+from concourse.masks import make_identity
+
+K, M, T, S = 512, 256, 2048, 512
+FLOPS = 2 * (2 * K * M * S)
+
+F32 = mybir.dt.float32
+BF16 = mybir.dt.bfloat16
+I32 = mybir.dt.int32
+U32 = mybir.dt.uint32
+U16 = mybir.dt.uint16
+U8 = mybir.dt.uint8
+FP8X4 = mybir.dt.float8_e4m3fn_x4
+FP4X4 = mybir.dt.float4_e2m1fn_x4
+ADD = mybir.AluOpType.add
+MULT = mybir.AluOpType.mult
+
+P = 128
+PACK = 4
+HALF = 256
+BLOCK = 128
+N_BLOCKS = S // BLOCK
+N_COLS = 128
+
+
+def tile_list_heads_tm_bias_kernel(
+    tc, xT, w4_words, w4_scales, r8_words, r8_scales, wgt, b, offs, out
+):
+    nc = tc.nc
+    with ExitStack() as ctx:
+        keep = ctx.enter_context(tc.tile_pool(name="keep", bufs=1))
+        psum = ctx.enter_context(tc.psum_pool(name="psum", bufs=1))
+
+        offsets = keep.tile([P, S // 16], U16, name="offsets")
+        nc.sync.dma_start(offsets[:], offs)
+        planes = [keep.tile([P, T], F32, name=f"plane{i}") for i in range(PACK)]
+        weight = keep.tile([P, S], F32, name="weight")
+        x_rows = xT.rearrange("(p i) t -> p i t", i=PACK)
+        nc.sync.dma_start(out=planes[0][:], in_=x_rows[:, 0, :])
+        nc.sync.dma_start(out=weight[:], in_=wgt)
+        for i in range(1, PACK):
+            nc.sync.dma_start(out=planes[i][:], in_=x_rows[:, i, :])
+        w4 = keep.tile([P, 2 * M], U8, name="w4", align_bytes=64)
+        nc.sync.dma_start(out=w4[:].bitcast(I32), in_=w4_words[0].bitcast(I32))
+        r8 = keep.tile([P, M], U32, name="r8", align_bytes=64)
+        nc.sync.dma_start(
+            out=r8[:].bitcast(I32), in_=r8_words[0].rearrange("p n i -> p (n i)").bitcast(I32)
+        )
+
+        b_pairs = keep.tile([P, 2], F32, name="b_pairs")
+        nc.gpsimd.dma_start(out=b_pairs[:], in_=b.rearrange("(p c) -> p c", c=2))
+        w4_sc = keep.tile([P, M], U8, name="w4_sc", align_bytes=64)
+        r8_sc = keep.tile([P, M], U8, name="r8_sc", align_bytes=64)
+        nc.vector.memset(w4_sc[:].bitcast(I32), 0)
+        nc.vector.memset(r8_sc[:].bitcast(I32), 0)
+        for q in range(4):
+            rows, live = slice(4 * q, 4 * q + 4), slice(32 * q, 32 * q + 4)
+            nc.scalar.dma_start(out=w4_sc[live, :].bitcast(I32), in_=w4_scales[0, rows, :].bitcast(I32))
+            nc.gpsimd.dma_start(out=r8_sc[live, :].bitcast(I32), in_=r8_scales[0, rows, :].bitcast(I32))
+
+        ident = keep.tile([P, P], F32, name="ident")
+        make_identity(nc, ident[:])
+        bias_bank = psum.tile([P, 2, P], F32, name="bias_bank")
+        for c in range(2):
+            nc.tensor.transpose(bias_bank[:, c, :], b_pairs[:, c : c + 1].to_broadcast([P, P]), ident[:])
+        bias = keep.tile([P, M], F32, name="bias")
+        nc.scalar.copy(
+            out=bias[:].rearrange("m (p c) -> m p c", c=2), in_=bias_bank[:].rearrange("m c p -> m p c")
+        )
+
+        picked = [keep.tile([P, PACK, HALF], F32, name=f"picked{h}") for h in range(2)]
+        rounded = [keep.tile([P, BLOCK, PACK], BF16, name=f"rounded{c}", align_bytes=64) for c in range(N_BLOCKS)]
+        codes = [keep.tile([P, BLOCK], U32, name=f"codes{c}", align_bytes=64) for c in range(N_BLOCKS)]
+        scales = [keep.tile([P, BLOCK], U8, name=f"scales{c}", align_bytes=64) for c in range(N_BLOCKS)]
+
+        def gather(i, j0, n):
+            h, at = divmod(j0, HALF)
+            nc.vector.tensor_tensor(
+                picked[h][:, i, at : at + n],
+                planes[i][:].indirect(offsets[:, j0 // 16 : (j0 + n) // 16]),
+                weight[:, j0 : j0 + n],
+                MULT,
+            )
+
+        def round_pair(copy, c, i):
+            h, at = divmod(c * BLOCK, HALF)
+            copy(
+                out=rounded[c][:, :, i : i + 2],
+                in_=picked[h][:, i : i + 2, at : at + BLOCK].rearrange("p i j -> p j i"),
+            )
+
+        for i in range(3):
+            for h in range(2):
+                gather(i, h * HALF, HALF)
+            if i == 1:
+                for c in range(N_BLOCKS):
+                    round_pair(nc.scalar.copy, c, 0)
+        for c in range(N_BLOCKS):
+            gather(3, c * BLOCK, BLOCK)
+            round_pair(nc.scalar.copy if c < 3 else nc.vector.tensor_copy, c, 2)
+        for c in range(N_BLOCKS):
+            nc.vector.quantize_mx(
+                out=codes[c][:].bitcast(FP8X4),
+                scales=scales[c][:],
+                in_=rounded[c][:].rearrange("p j i -> p (j i)"),
+            )
+            bank = psum.tile([P, M], F32, name=f"bank{c}")
+            for n0 in range(0, M, N_COLS):
+                cols = slice(n0, n0 + N_COLS)
+                nc.tensor.matmul_mx(
+                    out=bank[:, cols],
+                    lhsT=codes[c][:].bitcast(FP8X4),
+                    lhsT_scale=scales[c][:],
+                    rhs=w4[:, 2 * n0 : 2 * (n0 + N_COLS)].bitcast(FP4X4),
+                    rhs_scale=w4_sc[:, cols],
+                    start=True,
+                    stop=False,
+                )
+                nc.tensor.matmul_mx(
+                    out=bank[:, cols],
+                    lhsT=codes[c][:].bitcast(FP8X4),
+                    lhsT_scale=scales[c][:],
+                    rhs=r8[:, cols].bitcast(FP8X4),
+                    rhs_scale=r8_sc[:, cols],
+                    start=False,
+                    stop=True,
+                )
+            result = keep.tile([P, M], F32, name=f"result{c}")
+            nc.vector.tensor_tensor(result[:], bank[:], bias[:], ADD)
+            nc.sync.dma_start(out=out[c * BLOCK : (c + 1) * BLOCK, :], in_=result[:])

@@ -34,11 +34,11 @@ def tile_list_heads_tm_bias_kernel(
         psum = ctx.enter_context(tc.psum_pool(name="psum", bufs=1))
 
         offsets = keep.tile([P, S // 16], U16, name="offsets")
-        nc.sync.dma_start(offsets[:], offs)
         planes = [keep.tile([P, T], F32, name=f"plane{i}") for i in range(PACK)]
         weight = keep.tile([P, S], F32, name="weight")
         x_rows = xT.rearrange("(p i) t -> p i t", i=PACK)
         nc.sync.dma_start(out=planes[0][:], in_=x_rows[:, 0, :])
+        nc.sync.dma_start(offsets[:], offs)
         nc.sync.dma_start(out=weight[:], in_=wgt)
         for i in range(1, PACK):
             nc.sync.dma_start(out=planes[i][:], in_=x_rows[:, i, :])
@@ -49,17 +49,17 @@ def tile_list_heads_tm_bias_kernel(
             out=r8[:].bitcast(I32), in_=r8_words[0].rearrange("p n i -> p (n i)").bitcast(I32)
         )
 
-        b_pairs = keep.tile([P, 2], F32, name="b_pairs")
-        nc.gpsimd.dma_start(out=b_pairs[:], in_=b.rearrange("(p c) -> p c", c=2))
         w4_sc = keep.tile([P, M], U8, name="w4_sc", align_bytes=64)
         r8_sc = keep.tile([P, M], U8, name="r8_sc", align_bytes=64)
-        nc.vector.memset(w4_sc[:].bitcast(I32), 0)
-        nc.vector.memset(r8_sc[:].bitcast(I32), 0)
+        nc.gpsimd.memset(w4_sc[:].bitcast(I32), 0)
+        nc.gpsimd.memset(r8_sc[:].bitcast(I32), 0)
         for q in range(4):
             rows, live = slice(4 * q, 4 * q + 4), slice(32 * q, 32 * q + 4)
             nc.scalar.dma_start(out=w4_sc[live, :].bitcast(I32), in_=w4_scales[0, rows, :].bitcast(I32))
             nc.gpsimd.dma_start(out=r8_sc[live, :].bitcast(I32), in_=r8_scales[0, rows, :].bitcast(I32))
 
+        b_pairs = keep.tile([P, 2], F32, name="b_pairs")
+        nc.gpsimd.dma_start(out=b_pairs[:], in_=b.rearrange("(p c) -> p c", c=2))
         ident = keep.tile([P, P], F32, name="ident")
         make_identity(nc, ident[:])
         bias_bank = psum.tile([P, 2, P], F32, name="bias_bank")
@@ -74,6 +74,12 @@ def tile_list_heads_tm_bias_kernel(
         rounded = [keep.tile([P, BLOCK, PACK], BF16, name=f"rounded{c}", align_bytes=64) for c in range(N_BLOCKS)]
         codes = [keep.tile([P, BLOCK], U32, name=f"codes{c}", align_bytes=64) for c in range(N_BLOCKS)]
         scales = [keep.tile([P, BLOCK], U8, name=f"scales{c}", align_bytes=64) for c in range(N_BLOCKS)]
+
+        warm_bank = psum.tile([P, 4, P], F32, name="warm_bank")
+
+        def warm(i, count):
+            for u in range(count):
+                nc.tensor.transpose(warm_bank[:, u % 4, :], planes[i][:, u * P : (u + 1) * P], ident[:])
 
         def gather(i, j0, n):
             h, at = divmod(j0, HALF)
@@ -94,13 +100,15 @@ def tile_list_heads_tm_bias_kernel(
         for i in range(3):
             for h in range(2):
                 gather(i, h * HALF, HALF)
+            if i == 2:
+                warm(2, 14)
             if i == 1:
                 for c in range(N_BLOCKS):
                     round_pair(nc.scalar.copy, c, 0)
+        warm(3, 8)
         for c in range(N_BLOCKS):
             gather(3, c * BLOCK, BLOCK)
             round_pair(nc.scalar.copy if c < 3 else nc.vector.tensor_copy, c, 2)
-        for c in range(N_BLOCKS):
             nc.vector.quantize_mx(
                 out=codes[c][:].bitcast(FP8X4),
                 scales=scales[c][:],

@@ -36,27 +36,31 @@ def tile_list_heads_tm_bias_kernel(
         offsets = keep.tile([P, S // 16], U16, name="offsets")
         planes = [keep.tile([P, T], F32, name=f"plane{i}") for i in range(PACK)]
         weight = keep.tile([P, S], F32, name="weight")
+        w4 = keep.tile([P, 2 * M], U8, name="w4", align_bytes=64)
+        r8 = keep.tile([P, M], U32, name="r8", align_bytes=64)
+        w4_sc = keep.tile([P, M], U8, name="w4_sc", align_bytes=64)
+        r8_sc = keep.tile([P, M], U8, name="r8_sc", align_bytes=64)
         x_rows = xT.rearrange("(p i) t -> p i t", i=PACK)
+
+        def load_scales(tile, source):
+            for q in range(4):
+                nc.sync.dma_start(
+                    out=tile[32 * q : 32 * q + 4, :].bitcast(I32),
+                    in_=source[0, 4 * q : 4 * q + 4, :].bitcast(I32),
+                )
+
         nc.sync.dma_start(out=planes[0][:], in_=x_rows[:, 0, :])
         nc.sync.dma_start(offsets[:], offs)
+        load_scales(w4_sc, w4_scales)
         nc.sync.dma_start(out=weight[:], in_=wgt)
-        for i in range(1, PACK):
-            nc.sync.dma_start(out=planes[i][:], in_=x_rows[:, i, :])
-        w4 = keep.tile([P, 2 * M], U8, name="w4", align_bytes=64)
+        nc.sync.dma_start(out=planes[1][:], in_=x_rows[:, 1, :])
+        nc.sync.dma_start(out=planes[2][:], in_=x_rows[:, 2, :])
+        load_scales(r8_sc, r8_scales)
+        nc.sync.dma_start(out=planes[3][:], in_=x_rows[:, 3, :])
         nc.sync.dma_start(out=w4[:].bitcast(I32), in_=w4_words[0].bitcast(I32))
-        r8 = keep.tile([P, M], U32, name="r8", align_bytes=64)
         nc.sync.dma_start(
             out=r8[:].bitcast(I32), in_=r8_words[0].rearrange("p n i -> p (n i)").bitcast(I32)
         )
-
-        w4_sc = keep.tile([P, M], U8, name="w4_sc", align_bytes=64)
-        r8_sc = keep.tile([P, M], U8, name="r8_sc", align_bytes=64)
-        nc.gpsimd.memset(w4_sc[:].bitcast(I32), 0)
-        nc.gpsimd.memset(r8_sc[:].bitcast(I32), 0)
-        for q in range(4):
-            rows, live = slice(4 * q, 4 * q + 4), slice(32 * q, 32 * q + 4)
-            nc.scalar.dma_start(out=w4_sc[live, :].bitcast(I32), in_=w4_scales[0, rows, :].bitcast(I32))
-            nc.gpsimd.dma_start(out=r8_sc[live, :].bitcast(I32), in_=r8_scales[0, rows, :].bitcast(I32))
 
         b_pairs = keep.tile([P, 2], F32, name="b_pairs")
         nc.gpsimd.dma_start(out=b_pairs[:], in_=b.rearrange("(p c) -> p c", c=2))
@@ -100,15 +104,15 @@ def tile_list_heads_tm_bias_kernel(
         for i in range(3):
             for h in range(2):
                 gather(i, h * HALF, HALF)
-            if i == 2:
-                warm(2, 14)
+            if i > 0:
+                warm(i, 16)
             if i == 1:
                 for c in range(N_BLOCKS):
                     round_pair(nc.scalar.copy, c, 0)
         warm(3, 8)
         for c in range(N_BLOCKS):
             gather(3, c * BLOCK, BLOCK)
-            round_pair(nc.scalar.copy if c < 3 else nc.vector.tensor_copy, c, 2)
+            round_pair(nc.scalar.copy, c, 2)
             nc.vector.quantize_mx(
                 out=codes[c][:].bitcast(FP8X4),
                 scales=scales[c][:],

@@ -79,12 +79,6 @@ def tile_list_heads_tm_bias_kernel(
         codes = [keep.tile([P, BLOCK], U32, name=f"codes{c}", align_bytes=64) for c in range(N_BLOCKS)]
         scales = [keep.tile([P, BLOCK], U8, name=f"scales{c}", align_bytes=64) for c in range(N_BLOCKS)]
 
-        warm_bank = psum.tile([P, 4, P], F32, name="warm_bank")
-
-        def warm(i, count):
-            for u in range(count):
-                nc.tensor.transpose(warm_bank[:, u % 4, :], planes[i][:, u * P : (u + 1) * P], ident[:])
-
         def gather(i, j0, n):
             h, at = divmod(j0, HALF)
             nc.vector.tensor_tensor(
@@ -104,12 +98,9 @@ def tile_list_heads_tm_bias_kernel(
         for i in range(3):
             for h in range(2):
                 gather(i, h * HALF, HALF)
-            if i > 0:
-                warm(i, 16)
             if i == 1:
                 for c in range(N_BLOCKS):
                     round_pair(nc.scalar.copy, c, 0)
-        warm(3, 8)
         for c in range(N_BLOCKS):
             gather(3, c * BLOCK, BLOCK)
             round_pair(nc.scalar.copy, c, 2)
@@ -118,27 +109,32 @@ def tile_list_heads_tm_bias_kernel(
                 scales=scales[c][:],
                 in_=rounded[c][:].rearrange("p j i -> p (j i)"),
             )
-            bank = psum.tile([P, M], F32, name=f"bank{c}")
-            for n0 in range(0, M, N_COLS):
-                cols = slice(n0, n0 + N_COLS)
-                nc.tensor.matmul_mx(
-                    out=bank[:, cols],
-                    lhsT=codes[c][:].bitcast(FP8X4),
-                    lhsT_scale=scales[c][:],
-                    rhs=w4[:, 2 * n0 : 2 * (n0 + N_COLS)].bitcast(FP4X4),
-                    rhs_scale=w4_sc[:, cols],
-                    start=True,
-                    stop=False,
-                )
-                nc.tensor.matmul_mx(
-                    out=bank[:, cols],
-                    lhsT=codes[c][:].bitcast(FP8X4),
-                    lhsT_scale=scales[c][:],
-                    rhs=r8[:, cols].bitcast(FP8X4),
-                    rhs_scale=r8_sc[:, cols],
-                    start=False,
-                    stop=True,
-                )
-            result = keep.tile([P, M], F32, name=f"result{c}")
-            nc.vector.tensor_tensor(result[:], bank[:], bias[:], ADD)
-            nc.sync.dma_start(out=out[c * BLOCK : (c + 1) * BLOCK, :], in_=result[:])
+            split = 2 if c == N_BLOCKS - 1 else 1
+            width = M // split
+            for s in range(split):
+                bank = psum.tile([P, width], F32, name=f"bank{c}_{s}")
+                for at in range(0, width, N_COLS):
+                    n0 = s * width + at
+                    cols = slice(n0, n0 + N_COLS)
+                    nc.tensor.matmul_mx(
+                        out=bank[:, at : at + N_COLS],
+                        lhsT=codes[c][:].bitcast(FP8X4),
+                        lhsT_scale=scales[c][:],
+                        rhs=w4[:, 2 * n0 : 2 * (n0 + N_COLS)].bitcast(FP4X4),
+                        rhs_scale=w4_sc[:, cols],
+                        start=True,
+                        stop=False,
+                    )
+                    nc.tensor.matmul_mx(
+                        out=bank[:, at : at + N_COLS],
+                        lhsT=codes[c][:].bitcast(FP8X4),
+                        lhsT_scale=scales[c][:],
+                        rhs=r8[:, cols].bitcast(FP8X4),
+                        rhs_scale=r8_sc[:, cols],
+                        start=False,
+                        stop=True,
+                    )
+                out_cols = slice(s * width, (s + 1) * width)
+                result = keep.tile([P, width], F32, name=f"result{c}_{s}")
+                nc.vector.tensor_tensor(result[:], bank[:], bias[:, out_cols], ADD)
+                nc.sync.dma_start(out=out[c * BLOCK : (c + 1) * BLOCK, out_cols], in_=result[:])

from contextlib import ExitStack

import concourse.mybir as mybir
from concourse.masks import make_identity

K, M, T, S = 512, 256, 2048, 512
FLOPS = 2 * (2 * K * M * S)

F32 = mybir.dt.float32
BF16 = mybir.dt.bfloat16
I32 = mybir.dt.int32
U32 = mybir.dt.uint32
U16 = mybir.dt.uint16
U8 = mybir.dt.uint8
FP8X4 = mybir.dt.float8_e4m3fn_x4
FP4X4 = mybir.dt.float4_e2m1fn_x4
ADD = mybir.AluOpType.add
MULT = mybir.AluOpType.mult

P = 128
PACK = 4
HALF = 256
BLOCK = 128
N_BLOCKS = S // BLOCK
N_COLS = 128


def tile_list_heads_tm_bias_kernel(
    tc, xT, w4_words, w4_scales, r8_words, r8_scales, wgt, b, offs, out
):
    nc = tc.nc
    with ExitStack() as ctx:
        keep = ctx.enter_context(tc.tile_pool(name="keep", bufs=1))
        psum = ctx.enter_context(tc.psum_pool(name="psum", bufs=1))

        offsets = keep.tile([P, S // 16], U16, name="offsets")
        planes = [keep.tile([P, T], F32, name=f"plane{i}") for i in range(PACK)]
        weight = keep.tile([P, S], F32, name="weight")
        w4 = keep.tile([P, 2 * M], U8, name="w4", align_bytes=64)
        r8 = keep.tile([P, M], U32, name="r8", align_bytes=64)
        w4_sc = keep.tile([P, M], U8, name="w4_sc", align_bytes=64)
        r8_sc = keep.tile([P, M], U8, name="r8_sc", align_bytes=64)
        x_rows = xT.rearrange("(p i) t -> p i t", i=PACK)

        def load_scales(tile, source):
            for q in range(4):
                nc.sync.dma_start(
                    out=tile[32 * q : 32 * q + 4, :].bitcast(I32),
                    in_=source[0, 4 * q : 4 * q + 4, :].bitcast(I32),
                )

        nc.sync.dma_start(out=planes[0][:], in_=x_rows[:, 0, :])
        nc.sync.dma_start(offsets[:], offs)
        load_scales(w4_sc, w4_scales)
        nc.sync.dma_start(out=weight[:], in_=wgt)
        nc.sync.dma_start(out=planes[1][:], in_=x_rows[:, 1, :])
        nc.sync.dma_start(out=planes[2][:], in_=x_rows[:, 2, :])
        load_scales(r8_sc, r8_scales)
        nc.sync.dma_start(out=planes[3][:], in_=x_rows[:, 3, :])
        nc.sync.dma_start(out=w4[:].bitcast(I32), in_=w4_words[0].bitcast(I32))
        nc.sync.dma_start(
            out=r8[:].bitcast(I32), in_=r8_words[0].rearrange("p n i -> p (n i)").bitcast(I32)
        )

        b_pairs = keep.tile([P, 2], F32, name="b_pairs")
        nc.gpsimd.dma_start(out=b_pairs[:], in_=b.rearrange("(p c) -> p c", c=2))
        ident = keep.tile([P, P], F32, name="ident")
        make_identity(nc, ident[:])
        bias_bank = psum.tile([P, 2, P], F32, name="bias_bank")
        for c in range(2):
            nc.tensor.transpose(bias_bank[:, c, :], b_pairs[:, c : c + 1].to_broadcast([P, P]), ident[:])
        bias = keep.tile([P, M], F32, name="bias")
        nc.scalar.copy(
            out=bias[:].rearrange("m (p c) -> m p c", c=2), in_=bias_bank[:].rearrange("m c p -> m p c")
        )

        picked = [keep.tile([P, PACK, HALF], F32, name=f"picked{h}") for h in range(2)]
        rounded = [keep.tile([P, BLOCK, PACK], BF16, name=f"rounded{c}", align_bytes=64) for c in range(N_BLOCKS)]
        codes = [keep.tile([P, BLOCK], U32, name=f"codes{c}", align_bytes=64) for c in range(N_BLOCKS)]
        scales = [keep.tile([P, BLOCK], U8, name=f"scales{c}", align_bytes=64) for c in range(N_BLOCKS)]

        def gather(i, j0, n):
            h, at = divmod(j0, HALF)
            nc.vector.tensor_tensor(
                picked[h][:, i, at : at + n],
                planes[i][:].indirect(offsets[:, j0 // 16 : (j0 + n) // 16]),
                weight[:, j0 : j0 + n],
                MULT,
            )

        def round_pair(copy, c, i):
            h, at = divmod(c * BLOCK, HALF)
            copy(
                out=rounded[c][:, :, i : i + 2],
                in_=picked[h][:, i : i + 2, at : at + BLOCK].rearrange("p i j -> p j i"),
            )

        for i in range(3):
            for h in range(2):
                gather(i, h * HALF, HALF)
            if i == 1:
                for c in range(N_BLOCKS):
                    round_pair(nc.scalar.copy, c, 0)
        for c in range(N_BLOCKS):
            gather(3, c * BLOCK, BLOCK)
            round_pair(nc.scalar.copy, c, 2)
            nc.vector.quantize_mx(
                out=codes[c][:].bitcast(FP8X4),
                scales=scales[c][:],
                in_=rounded[c][:].rearrange("p j i -> p (j i)"),
            )
            split = 2 if c == N_BLOCKS - 1 else 1
            width = M // split
            for s in range(split):
                bank = psum.tile([P, width], F32, name=f"bank{c}_{s}")
                for at in range(0, width, N_COLS):
                    n0 = s * width + at
                    cols = slice(n0, n0 + N_COLS)
                    nc.tensor.matmul_mx(
                        out=bank[:, at : at + N_COLS],
                        lhsT=codes[c][:].bitcast(FP8X4),
                        lhsT_scale=scales[c][:],
                        rhs=w4[:, 2 * n0 : 2 * (n0 + N_COLS)].bitcast(FP4X4),
                        rhs_scale=w4_sc[:, cols],
                        start=True,
                        stop=False,
                    )
                    nc.tensor.matmul_mx(
                        out=bank[:, at : at + N_COLS],
                        lhsT=codes[c][:].bitcast(FP8X4),
                        lhsT_scale=scales[c][:],
                        rhs=r8[:, cols].bitcast(FP8X4),
                        rhs_scale=r8_sc[:, cols],
                        start=False,
                        stop=True,
                    )
                out_cols = slice(s * width, (s + 1) * width)
                result = keep.tile([P, width], F32, name=f"result{c}_{s}")
                nc.vector.tensor_tensor(result[:], bank[:], bias[:, out_cols], ADD)
                nc.sync.dma_start(out=out[c * BLOCK : (c + 1) * BLOCK, out_cols], in_=result[:])
